import numpy as np
import ml_dtypes


def mxq(x, axis, fmt="e4m3"):
    dtype, down = {"e4m3": (ml_dtypes.float8_e4m3fn, 7), "e5m2": (ml_dtypes.float8_e5m2, 14)}[fmt]
    v = np.moveaxis(np.asarray(x, np.float32).astype(ml_dtypes.bfloat16).astype(np.float64), axis, -1)
    blocks = v.reshape(v.shape[:-1] + (-1, 32))
    amax = np.abs(blocks).max(-1, keepdims=True)
    byte = np.maximum(np.where(amax > 0, np.frexp(amax)[1] - 1 + 127, 0) - down, 1)
    scale = np.exp2(byte - 127.0)
    codes = (blocks / scale).astype(np.float32).astype(dtype).astype(np.float64)
    return np.moveaxis((codes * scale).reshape(v.shape), -1, axis)


WIDE = False


def mx_kscale(k):
    if not WIDE:
        return np.ones(k)
    levels = np.array([10, -10, 5, -5, 0])
    if k % 512:
        return np.exp2(np.random.permutation(np.resize(levels, k // 32))).repeat(32)
    a = np.empty((k // 512, 16))
    for p in range(k // 512):
        a[p, :8] = np.random.permutation(np.resize(levels, 8))
        for g in range(8):
            far = levels[np.abs(levels - a[p, g]) >= 10]
            a[p, g + 8] = far[np.random.randint(len(far))]
    return np.exp2(a.ravel()).repeat(32)


def f64(x):
    return np.asarray(x).astype(np.float64)


def striped(idx):
    return np.tile(idx.reshape(-1, 16).T, (8, 1)).astype(np.uint16)


def unstriped(offs):
    return offs[:16].T.reshape(-1).astype(np.int64)


def relu(v):
    return np.maximum(v, 0.0)


K, T, H, N = 512, 256, 512, 256


def setup_inputs():
    n = np.random.standard_normal
    s = mx_kscale(K)[:, None]
    u = mx_kscale(H)
    idx = np.random.permutation(H)
    v = np.empty(H)
    v[idx] = u
    return {
        "xT": (n((K, T)) * s).astype(np.float32),
        "w1": (n((K, H)) / np.sqrt(K) / s * v).astype(np.float32),
        "w2": (n((H, N)) / np.sqrt(H) / u[:, None]).astype(np.float32),
        "offs": striped(idx),
    }


def reference(xT, w1, w2, offs):
    idx = unstriped(offs)
    h = relu(mxq(f64(w1), 0, "e4m3").T @ mxq(f64(xT), 0, "e4m3"))
    return mxq(f64(w2), 0, "e4m3").T @ mxq(h[idx], 0, "e4m3")

@@ -1,0 +1,121 @@
+from contextlib import ExitStack
+
+import concourse.mybir as mybir
+from concourse.masks import make_identity
+
+K, T, H, N = 512, 256, 512, 256
+P = 128
+PACK = 4
+FLOPS = 2 * K * H * T + 2 * H * N * T
+
+F32 = mybir.dt.float32
+BF16 = mybir.dt.bfloat16
+U32 = mybir.dt.uint32
+U16 = mybir.dt.uint16
+U8 = mybir.dt.uint8
+FP8X4 = mybir.dt.float8_e4m3fn_x4
+RELU = mybir.ActivationFunctionType.Relu
+COPY = mybir.ActivationFunctionType.Copy
+
+
+def tile_picked_shuffle_mlp_relu_perm_l_kernel(tc, xT, w1, w2, offs, out):
+    nc = tc.nc
+    with ExitStack() as ctx:
+        keep = ctx.enter_context(tc.tile_pool(name="keep", bufs=1))
+        psum = ctx.enter_context(tc.psum_pool(name="psum", bufs=1))
+
+        offsets = keep.tile([P, H // 16], U16, name="offsets")
+
+        w1_rows = w1.rearrange("(p j) c -> p j c", j=PACK)
+        w1_raw = []
+        for u in range(2):
+            half = keep.tile([P, 2, H], F32, name=f"w1_raw{u}", tag=["early", "late"][u])
+            nc.sync.dma_start(out=half[:], in_=w1_rows[:, 2 * u : 2 * u + 2, :])
+            w1_raw.append(half)
+        x_raw = keep.tile([P, PACK, T], F32, name="x_raw")
+        nc.sync.dma_start(out=x_raw[:], in_=xT.rearrange("(p j) t -> p j t", j=PACK))
+        nc.sync.dma_start(offsets[:], offs)
+
+        spark = keep.tile([P, 1], F32, name="spark")
+        nc.vector.memset(spark[:], 0.0)
+        spark_out = keep.tile([P, 1], F32, name="spark_out")
+        nc.scalar.activation(spark_out[:], spark[:], RELU)
+        ident = keep.tile([P, P], F32, name="ident")
+        make_identity(nc, ident[:])
+
+        w1_g = keep.tile([P, H, PACK], BF16, name="w1_g", align_bytes=64)
+        w1_codes = keep.tile([P, H], U32, name="w1_codes", align_bytes=64)
+        w1_scales = keep.tile([P, H], U8, name="w1_scales", align_bytes=64)
+        x_g = keep.tile([P, T, PACK], BF16, name="x_g", align_bytes=64)
+        x_codes = keep.tile([P, T], U32, name="x_codes", align_bytes=64)
+        x_scales = keep.tile([P, T], U8, name="x_scales", align_bytes=64)
+
+        def interleave(grouped, raw, js, split):
+            for engine_copy, cols in zip((nc.vector.tensor_copy, nc.scalar.copy, nc.scalar.copy), split):
+                engine_copy(grouped[:, cols[0] : cols[1], js], raw[:, :, cols[0] : cols[1]].rearrange("p j c -> p c j"))
+
+        def quantise(codes, scales, grouped, cols):
+            nc.vector.quantize_mx(out=codes[:, cols].bitcast(FP8X4), scales=scales[:, cols], in_=grouped[:, cols, :].rearrange("p c j -> p (c j)"))
+
+        def block(i, width=P):
+            return slice(i * width, (i + 1) * width)
+
+        interleave(w1_g, w1_raw[0], slice(0, 2), [(0, 344), (344, 512)])
+        interleave(w1_g, w1_raw[1], slice(2, 4), [(0, 256), (256, 512)])
+        w2_raw = keep.tile([P, PACK, N], F32, name="w2_raw", tag="late")
+        nc.sync.dma_start(out=w2_raw[:], in_=w2.rearrange("(p j) m -> p j m", j=PACK))
+        quantise(w1_codes, w1_scales, w1_g, block(0, 256))
+        interleave(x_g, x_raw, slice(0, 4), [(0, 96), (96, 128), (128, 256)])
+        quantise(x_codes, x_scales, x_g, block(0))
+        quantise(w1_codes, w1_scales, w1_g, block(1, 256))
+        quantise(x_codes, x_scales, x_g, block(1))
+
+        h0 = keep.tile([P, H], F32, name="h0")
+        h1 = keep.tile([P, H], BF16, name="h1")
+        pieces = [(0, 0, 256), (0, 256, 512), (1, 0, 256), (1, 256, 384), (1, 384, 512)]
+        for i, (e, c0, c1) in enumerate(pieces):
+            prod = psum.tile([P, c1 - c0], F32, name=f"prod{i}")
+            nc.tensor.matmul_mx(out=prod[:], lhsT=x_codes[:, block(e)].bitcast(FP8X4), lhsT_scale=x_scales[:, block(e)], rhs=w1_codes[:, c0:c1].bitcast(FP8X4), rhs_scale=w1_scales[:, c0:c1], start=True, stop=True)
+            if i in (0, 3):
+                nc.vector.tensor_scalar_max((h0, h1)[e][:, c0:c1], prod[:], 0.0)
+            else:
+                nc.scalar.activation((h0, h1)[e][:, c0:c1], prod[:], RELU)
+
+        picked = [keep.tile([P, 2, P, 2], BF16, name=f"picked{e}") for e in range(2)]
+        for a in range(2):
+            slots = [picked[e][:, :, 64 * a : 64 * a + 64, :].rearrange("p u m v -> p m u v") for e in range(2)]
+            listed = offsets[:, 16 * a : 16 * a + 16]
+            nc.vector.tensor_copy(slots[0], h0[:].indirect(listed))
+            nc.scalar.activation(slots[1], h1[:].indirect(listed), COPY)
+
+        w2_g = keep.tile([P, N, PACK], BF16, name="w2_g", align_bytes=64)
+        w2_codes = keep.tile([P, N], U32, name="w2_codes", align_bytes=64)
+        w2_scales = keep.tile([P, N], U8, name="w2_scales", align_bytes=64)
+        nc.vector.tensor_copy(w2_g[:], w2_raw[:].rearrange("p j m -> p m j"))
+        quantise(w2_codes, w2_scales, w2_g, block(0, N))
+
+        hq_g = keep.tile([P, T, PACK], BF16, name="hq_g", align_bytes=64)
+        h_codes = keep.tile([P, T], U32, name="h_codes", align_bytes=64)
+        h_scales = keep.tile([P, T], U8, name="h_scales", align_bytes=64)
+        for e in range(2):
+            turned = psum.tile([P, 2, P], F32, name=f"turned{e}")
+            for u in range(2):
+                nc.tensor.transpose(turned[:, u, :], picked[e][:, u, :, :].rearrange("p m v -> p (m v)").bitcast(F32), ident[:])
+            words = hq_g[:, block(e), :].rearrange("p n t -> p (n t)").bitcast(F32).rearrange("p (n u) -> p n u", u=2)
+            if e == 0:
+                nc.scalar.copy(words, turned[:].rearrange("p u n -> p n u"))
+            else:
+                nc.vector.tensor_copy(words, turned[:].rearrange("p u n -> p n u"))
+        out_rows = out.rearrange("(b m) t -> m b t", b=2)
+        for e in range(2):
+            ts = block(e)
+            quantise(h_codes, h_scales, hq_g, ts)
+            res = [psum.tile([P, P], F32, name=f"res{e}{b}", tag=f"prod{2 * e + b}") for b in range(2)]
+            for b in range(2):
+                ms = block(b)
+                nc.tensor.matmul_mx(out=res[b][:], lhsT=w2_codes[:, ms].bitcast(FP8X4), lhsT_scale=w2_scales[:, ms], rhs=h_codes[:, ts].bitcast(FP8X4), rhs_scale=h_scales[:, ts], start=True, stop=True)
+            done = [keep.tile([P, P], F32, name=f"done{e}{b}") for b in range(2)]
+            nc.scalar.copy(done[0][:], res[0][:])
+            nc.vector.tensor_copy(done[1][:], res[1][:])
+            nc.scalar.dma_start(out=out_rows[:, 0, ts], in_=done[0][:])
+            nc.sync.dma_start(out=out_rows[:, 1, ts], in_=done[1][:])

@@ -17,24 +17,29 @@ FP8X4 = mybir.dt.float8_e4m3fn_x4
 RELU = mybir.ActivationFunctionType.Relu
 COPY = mybir.ActivationFunctionType.Copy
 
+LIST_ON_VECTOR = (20, 16)
+
 
 def tile_picked_shuffle_mlp_relu_perm_l_kernel(tc, xT, w1, w2, offs, out):
     nc = tc.nc
     with ExitStack() as ctx:
         keep = ctx.enter_context(tc.tile_pool(name="keep", bufs=1))
+        shared = ctx.enter_context(tc.tile_pool(name="shared", bufs=1))
         psum = ctx.enter_context(tc.psum_pool(name="psum", bufs=1))
 
-        offsets = keep.tile([P, H // 16], U16, name="offsets")
+        def block(i, width=P):
+            return slice(i * width, (i + 1) * width)
 
+        offsets = keep.tile([P, H // 16], U16, name="offsets")
         w1_rows = w1.rearrange("(p j) c -> p j c", j=PACK)
-        w1_raw = []
+        w1_raw = [keep.tile([P, 2, H], F32, name=f"w1_raw{u}") for u in range(2)]
         for u in range(2):
-            half = keep.tile([P, 2, H], F32, name=f"w1_raw{u}", tag=["early", "late"][u])
-            nc.sync.dma_start(out=half[:], in_=w1_rows[:, 2 * u : 2 * u + 2, :])
-            w1_raw.append(half)
+            nc.sync.dma_start(out=w1_raw[u][:], in_=w1_rows[:, block(u, 2), :])
         x_raw = keep.tile([P, PACK, T], F32, name="x_raw")
         nc.sync.dma_start(out=x_raw[:], in_=xT.rearrange("(p j) t -> p j t", j=PACK))
         nc.sync.dma_start(offsets[:], offs)
+        w2_raw = shared.tile([P, PACK, N], F32, name="w2_raw", offset=0, align_bytes=64)
+        nc.sync.dma_start(out=w2_raw[:], in_=w2.rearrange("(p j) m -> p j m", j=PACK))
 
         spark = keep.tile([P, 1], F32, name="spark")
         nc.vector.memset(spark[:], 0.0)
@@ -43,79 +48,68 @@ def tile_picked_shuffle_mlp_relu_perm_l_kernel(tc, xT, w1, w2, offs, out):
         ident = keep.tile([P, P], F32, name="ident")
         make_identity(nc, ident[:])
 
-        w1_g = keep.tile([P, H, PACK], BF16, name="w1_g", align_bytes=64)
-        w1_codes = keep.tile([P, H], U32, name="w1_codes", align_bytes=64)
-        w1_scales = keep.tile([P, H], U8, name="w1_scales", align_bytes=64)
-        x_g = keep.tile([P, T, PACK], BF16, name="x_g", align_bytes=64)
-        x_codes = keep.tile([P, T], U32, name="x_codes", align_bytes=64)
-        x_scales = keep.tile([P, T], U8, name="x_scales", align_bytes=64)
+        def interleave(copy, grouped, raw, js, c0, c1):
+            copy(grouped[:, c0:c1, js].rearrange("p (c i) j -> p c j i", i=4), raw[:, :, c0:c1].rearrange("p j (c i) -> p c j i", i=4))
 
-        def interleave(grouped, raw, js, split):
-            for engine_copy, cols in zip((nc.vector.tensor_copy, nc.scalar.copy, nc.scalar.copy), split):
-                engine_copy(grouped[:, cols[0] : cols[1], js], raw[:, :, cols[0] : cols[1]].rearrange("p j c -> p c j"))
+        def mx_tiles(name, width):
+            grouped = keep.tile([P, width, PACK], BF16, name=f"{name}_grouped", align_bytes=64)
+            codes = keep.tile([P, width], U32, name=f"{name}_codes", align_bytes=64)
+            scales = keep.tile([P, width], U8, name=f"{name}_scales", align_bytes=64)
+            return grouped, codes, scales
 
-        def quantise(codes, scales, grouped, cols):
+        def quantise(mx, cols):
+            grouped, codes, scales = mx
             nc.vector.quantize_mx(out=codes[:, cols].bitcast(FP8X4), scales=scales[:, cols], in_=grouped[:, cols, :].rearrange("p c j -> p (c j)"))
 
-        def block(i, width=P):
-            return slice(i * width, (i + 1) * width)
+        def product(res, lhs, lhs_cols, rhs, rhs_cols):
+            nc.tensor.matmul_mx(out=res, lhsT=lhs[1][:, lhs_cols].bitcast(FP8X4), lhsT_scale=lhs[2][:, lhs_cols], rhs=rhs[1][:, rhs_cols].bitcast(FP8X4), rhs_scale=rhs[2][:, rhs_cols], start=True, stop=True)
 
-        interleave(w1_g, w1_raw[0], slice(0, 2), [(0, 344), (344, 512)])
-        interleave(w1_g, w1_raw[1], slice(2, 4), [(0, 256), (256, 512)])
-        w2_raw = keep.tile([P, PACK, N], F32, name="w2_raw", tag="late")
-        nc.sync.dma_start(out=w2_raw[:], in_=w2.rearrange("(p j) m -> p j m", j=PACK))
-        quantise(w1_codes, w1_scales, w1_g, block(0, 256))
-        interleave(x_g, x_raw, slice(0, 4), [(0, 96), (96, 128), (128, 256)])
-        quantise(x_codes, x_scales, x_g, block(0))
-        quantise(w1_codes, w1_scales, w1_g, block(1, 256))
-        quantise(x_codes, x_scales, x_g, block(1))
+        w1_mx = mx_tiles("w1", H)
+        x_mx = mx_tiles("x", T)
+        for u, on_vector in enumerate((344, 256)):
+            interleave(nc.vector.tensor_copy, w1_mx[0], w1_raw[u], block(u, 2), 0, on_vector)
+            interleave(nc.scalar.copy, w1_mx[0], w1_raw[u], block(u, 2), on_vector, H)
+        quantise(w1_mx, block(0, 256))
+        interleave(nc.vector.tensor_copy, x_mx[0], x_raw, block(0, PACK), 0, 96)
+        interleave(nc.scalar.copy, x_mx[0], x_raw, block(0, PACK), 96, P)
+        interleave(nc.scalar.copy, x_mx[0], x_raw, block(0, PACK), P, T)
+        quantise(x_mx, block(0))
+        quantise(w1_mx, block(1, 256))
+        quantise(x_mx, block(1))
 
-        h0 = keep.tile([P, H], F32, name="h0")
-        h1 = keep.tile([P, H], BF16, name="h1")
-        pieces = [(0, 0, 256), (0, 256, 512), (1, 0, 256), (1, 256, 384), (1, 384, 512)]
-        for i, (e, c0, c1) in enumerate(pieces):
-            prod = psum.tile([P, c1 - c0], F32, name=f"prod{i}")
-            nc.tensor.matmul_mx(out=prod[:], lhsT=x_codes[:, block(e)].bitcast(FP8X4), lhsT_scale=x_scales[:, block(e)], rhs=w1_codes[:, c0:c1].bitcast(FP8X4), rhs_scale=w1_scales[:, c0:c1], start=True, stop=True)
-            if i in (0, 3):
-                nc.vector.tensor_scalar_max((h0, h1)[e][:, c0:c1], prod[:], 0.0)
-            else:
-                nc.scalar.activation((h0, h1)[e][:, c0:c1], prod[:], RELU)
-
-        picked = [keep.tile([P, 2, P, 2], BF16, name=f"picked{e}") for e in range(2)]
-        for a in range(2):
-            slots = [picked[e][:, :, 64 * a : 64 * a + 64, :].rearrange("p u m v -> p m u v") for e in range(2)]
-            listed = offsets[:, 16 * a : 16 * a + 16]
-            nc.vector.tensor_copy(slots[0], h0[:].indirect(listed))
-            nc.scalar.activation(slots[1], h1[:].indirect(listed), COPY)
-
-        w2_g = keep.tile([P, N, PACK], BF16, name="w2_g", align_bytes=64)
-        w2_codes = keep.tile([P, N], U32, name="w2_codes", align_bytes=64)
-        w2_scales = keep.tile([P, N], U8, name="w2_scales", align_bytes=64)
-        nc.vector.tensor_copy(w2_g[:], w2_raw[:].rearrange("p j m -> p m j"))
-        quantise(w2_codes, w2_scales, w2_g, block(0, N))
-
-        hq_g = keep.tile([P, T, PACK], BF16, name="hq_g", align_bytes=64)
-        h_codes = keep.tile([P, T], U32, name="h_codes", align_bytes=64)
-        h_scales = keep.tile([P, T], U8, name="h_scales", align_bytes=64)
+        h = [keep.tile([P, H], BF16, name=f"h{e}") for e in range(2)]
         for e in range(2):
-            turned = psum.tile([P, 2, P], F32, name=f"turned{e}")
+            for a in range(2):
+                prod = psum.tile([P, H // 2], F32, name=f"prod{e}{a}", tag=f"bank{2 * e + a}")
+                product(prod[:], x_mx, block(e), w1_mx, block(a, H // 2))
+                nc.scalar.activation(h[e][:, block(a, H // 2)], prod[:], RELU)
+
+        w2_mx = mx_tiles("w2", N)
+        interleave(nc.vector.tensor_copy, w2_mx[0], w2_raw, block(0, PACK), 0, N)
+
+        picked = [shared.tile([P, H], BF16, name=f"picked{e}", offset=2 * H * e, align_bytes=64) for e in range(2)]
+        turned = [psum.tile([P, 2, P], F32, name=f"turned{e}", tag=f"bank{4 + e}") for e in range(2)]
+        for e in range(2):
+            cut = LIST_ON_VECTOR[e]
+            nc.vector.tensor_copy(picked[e][:, : 16 * cut], h[e][:].indirect(offsets[:, :cut]))
+            nc.scalar.activation(picked[e][:, 16 * cut :], h[e][:].indirect(offsets[:, cut:]), COPY)
             for u in range(2):
-                nc.tensor.transpose(turned[:, u, :], picked[e][:, u, :, :].rearrange("p m v -> p (m v)").bitcast(F32), ident[:])
-            words = hq_g[:, block(e), :].rearrange("p n t -> p (n t)").bitcast(F32).rearrange("p (n u) -> p n u", u=2)
-            if e == 0:
-                nc.scalar.copy(words, turned[:].rearrange("p u n -> p n u"))
-            else:
-                nc.vector.tensor_copy(words, turned[:].rearrange("p u n -> p n u"))
+                nc.tensor.transpose(turned[e][:, u, :], picked[e][:].bitcast(F32)[:, u : H // 2 : 2], ident[:])
+        quantise(w2_mx, block(0, N))
+
+        h_mx = [mx_tiles(f"h{e}", P) for e in range(2)]
+        for e in range(2):
+            words = h_mx[e][0][:].rearrange("p n t -> p (n t)").bitcast(F32).rearrange("p (n u) -> p n u", u=2)
+            nc.scalar.copy(words, turned[e][:].rearrange("p u n -> p n u"))
+
         out_rows = out.rearrange("(b m) t -> m b t", b=2)
         for e in range(2):
-            ts = block(e)
-            quantise(h_codes, h_scales, hq_g, ts)
-            res = [psum.tile([P, P], F32, name=f"res{e}{b}", tag=f"prod{2 * e + b}") for b in range(2)]
+            quantise(h_mx[e], block(0))
+            res = [psum.tile([P, P], F32, name=f"res{e}{b}", tag=f"bank{2 * e + b}") for b in range(2)]
             for b in range(2):
-                ms = block(b)
-                nc.tensor.matmul_mx(out=res[b][:], lhsT=w2_codes[:, ms].bitcast(FP8X4), lhsT_scale=w2_scales[:, ms], rhs=h_codes[:, ts].bitcast(FP8X4), rhs_scale=h_scales[:, ts], start=True, stop=True)
+                product(res[b][:], w2_mx, block(b), h_mx[e], block(0))
             done = [keep.tile([P, P], F32, name=f"done{e}{b}") for b in range(2)]
             nc.scalar.copy(done[0][:], res[0][:])
             nc.vector.tensor_copy(done[1][:], res[1][:])
-            nc.scalar.dma_start(out=out_rows[:, 0, ts], in_=done[0][:])
-            nc.sync.dma_start(out=out_rows[:, 1, ts], in_=done[1][:])
+            nc.scalar.dma_start(out=out_rows[:, 0, block(e)], in_=done[0][:])
+            nc.sync.dma_start(out=out_rows[:, 1, block(e)], in_=done[1][:])

@@ -17,7 +17,7 @@ FP8X4 = mybir.dt.float8_e4m3fn_x4
 RELU = mybir.ActivationFunctionType.Relu
 COPY = mybir.ActivationFunctionType.Copy
 
-LIST_ON_VECTOR = (20, 16)
+LIST_ON_VECTOR = (16, 16)
 
 
 def tile_picked_shuffle_mlp_relu_perm_l_kernel(tc, xT, w1, w2, offs, out):
@@ -32,11 +32,13 @@ def tile_picked_shuffle_mlp_relu_perm_l_kernel(tc, xT, w1, w2, offs, out):
 
         offsets = keep.tile([P, H // 16], U16, name="offsets")
         w1_rows = w1.rearrange("(p j) c -> p j c", j=PACK)
-        w1_raw = [keep.tile([P, 2, H], F32, name=f"w1_raw{u}") for u in range(2)]
-        for u in range(2):
-            nc.sync.dma_start(out=w1_raw[u][:], in_=w1_rows[:, block(u, 2), :])
+        w1_upper = keep.tile([P, 2, H], F32, name="w1_upper")
+        nc.sync.dma_start(out=w1_upper[:], in_=w1_rows[:, 0:2, :])
+        w1_lower = [keep.tile([P, 2, H // 2], F32, name=f"w1_lower{a}") for a in range(2)]
+        nc.sync.dma_start(out=w1_lower[0][:], in_=w1_rows[:, 2:4, block(0, H // 2)])
         x_raw = keep.tile([P, PACK, T], F32, name="x_raw")
         nc.sync.dma_start(out=x_raw[:], in_=xT.rearrange("(p j) t -> p j t", j=PACK))
+        nc.sync.dma_start(out=w1_lower[1][:], in_=w1_rows[:, 2:4, block(1, H // 2)])
         nc.sync.dma_start(offsets[:], offs)
         w2_raw = shared.tile([P, PACK, N], F32, name="w2_raw", offset=0, align_bytes=64)
         nc.sync.dma_start(out=w2_raw[:], in_=w2.rearrange("(p j) m -> p j m", j=PACK))
@@ -66,29 +68,37 @@ def tile_picked_shuffle_mlp_relu_perm_l_kernel(tc, xT, w1, w2, offs, out):
 
         w1_mx = mx_tiles("w1", H)
         x_mx = mx_tiles("x", T)
-        for u, on_vector in enumerate((344, 256)):
-            interleave(nc.vector.tensor_copy, w1_mx[0], w1_raw[u], block(u, 2), 0, on_vector)
-            interleave(nc.scalar.copy, w1_mx[0], w1_raw[u], block(u, 2), on_vector, H)
+        interleave(nc.vector.tensor_copy, w1_mx[0], w1_upper, block(0, 2), 0, 344)
+        interleave(nc.scalar.copy, w1_mx[0], w1_upper, block(0, 2), 344, H)
+        interleave(nc.vector.tensor_copy, w1_mx[0], w1_lower[0], block(1, 2), 0, 176)
+        interleave(nc.scalar.copy, w1_mx[0], w1_lower[0], block(1, 2), 176, 256)
         quantise(w1_mx, block(0, 256))
         interleave(nc.vector.tensor_copy, x_mx[0], x_raw, block(0, PACK), 0, 96)
         interleave(nc.scalar.copy, x_mx[0], x_raw, block(0, PACK), 96, P)
-        interleave(nc.scalar.copy, x_mx[0], x_raw, block(0, PACK), P, T)
+        interleave(nc.vector.tensor_copy, x_mx[0], x_raw, block(0, PACK), P, 192)
+        interleave(nc.scalar.copy, x_mx[0], x_raw, block(0, PACK), 192, T)
         quantise(x_mx, block(0))
-        quantise(w1_mx, block(1, 256))
+        right = w1_mx[0][:, block(1, H // 2), :]
+        interleave(nc.vector.tensor_copy, right, w1_lower[1], block(1, 2), 0, P)
+        interleave(nc.scalar.copy, right, w1_lower[1], block(1, 2), P, 2 * P)
         quantise(x_mx, block(1))
+        quantise(w1_mx, block(2))
+        quantise(w1_mx, block(3))
 
         h = [keep.tile([P, H], BF16, name=f"h{e}") for e in range(2)]
-        for e in range(2):
-            for a in range(2):
-                prod = psum.tile([P, H // 2], F32, name=f"prod{e}{a}", tag=f"bank{2 * e + a}")
-                product(prod[:], x_mx, block(e), w1_mx, block(a, H // 2))
-                nc.scalar.activation(h[e][:, block(a, H // 2)], prod[:], RELU)
+        spans = [slice(0, 256), slice(256, 384), slice(384, 512)]
+        prod = [[psum.tile([P, s.stop - s.start], F32, name=f"prod{e}{i}", tag=f"bank{3 * e + i}") for i, s in enumerate(spans)] for e in range(2)]
+        for i, s in enumerate(spans):
+            for e in range(2):
+                product(prod[e][i][:], x_mx, block(e), w1_mx, s)
+        for e, i in ((0, 0), (1, 0), (0, 1), (0, 2), (1, 1), (1, 2)):
+            nc.scalar.activation(h[e][:, spans[i]], prod[e][i][:], RELU)
 
         w2_mx = mx_tiles("w2", N)
         interleave(nc.vector.tensor_copy, w2_mx[0], w2_raw, block(0, PACK), 0, N)
 
         picked = [shared.tile([P, H], BF16, name=f"picked{e}", offset=2 * H * e, align_bytes=64) for e in range(2)]
-        turned = [psum.tile([P, 2, P], F32, name=f"turned{e}", tag=f"bank{4 + e}") for e in range(2)]
+        turned = [psum.tile([P, 2, P], F32, name=f"turned{e}", tag=f"bank{6 + e}") for e in range(2)]
         for e in range(2):
             cut = LIST_ON_VECTOR[e]
             nc.vector.tensor_copy(picked[e][:, : 16 * cut], h[e][:].indirect(offsets[:, :cut]))

@@ -43,10 +43,6 @@ def tile_picked_shuffle_mlp_relu_perm_l_kernel(tc, xT, w1, w2, offs, out):
         w2_raw = shared.tile([P, PACK, N], F32, name="w2_raw", offset=0, align_bytes=64)
         nc.sync.dma_start(out=w2_raw[:], in_=w2.rearrange("(p j) m -> p j m", j=PACK))
 
-        spark = keep.tile([P, 1], F32, name="spark")
-        nc.vector.memset(spark[:], 0.0)
-        spark_out = keep.tile([P, 1], F32, name="spark_out")
-        nc.scalar.activation(spark_out[:], spark[:], RELU)
         ident = keep.tile([P, P], F32, name="ident")
         make_identity(nc, ident[:])
 
@@ -87,12 +83,16 @@ def tile_picked_shuffle_mlp_relu_perm_l_kernel(tc, xT, w1, w2, offs, out):
 
         h = [keep.tile([P, H], BF16, name=f"h{e}") for e in range(2)]
         spans = [slice(0, 256), slice(256, 384), slice(384, 512)]
-        prod = [[psum.tile([P, s.stop - s.start], F32, name=f"prod{e}{i}", tag=f"bank{3 * e + i}") for i, s in enumerate(spans)] for e in range(2)]
+        prod0 = [psum.tile([P, s.stop - s.start], F32, name=f"prod0{i}", tag=f"bank{i}") for i, s in enumerate(spans)]
+        prod1 = [psum.tile([P, H // 2], F32, name=f"prod1{a}", tag=f"bank{3 + a}") for a in range(2)]
         for i, s in enumerate(spans):
-            for e in range(2):
-                product(prod[e][i][:], x_mx, block(e), w1_mx, s)
-        for e, i in ((0, 0), (1, 0), (0, 1), (0, 2), (1, 1), (1, 2)):
-            nc.scalar.activation(h[e][:, spans[i]], prod[e][i][:], RELU)
+            product(prod0[i][:], x_mx, block(0), w1_mx, s)
+            product(prod1[0][:] if i == 0 else prod1[1][:, block(i - 1)], x_mx, block(1), w1_mx, s)
+        nc.scalar.activation(h[0][:, spans[0]], prod0[0][:], RELU)
+        nc.scalar.activation(h[1][:, block(0, H // 2)], prod1[0][:], RELU)
+        nc.scalar.activation(h[0][:, spans[1]], prod0[1][:], RELU)
+        nc.scalar.activation(h[0][:, spans[2]], prod0[2][:], RELU)
+        nc.scalar.activation(h[1][:, block(1, H // 2)], prod1[1][:], RELU)
 
         w2_mx = mx_tiles("w2", N)
         interleave(nc.vector.tensor_copy, w2_mx[0], w2_raw, block(0, PACK), 0, N)

@@ -43,6 +43,10 @@ def tile_picked_shuffle_mlp_relu_perm_l_kernel(tc, xT, w1, w2, offs, out):
         w2_raw = shared.tile([P, PACK, N], F32, name="w2_raw", offset=0, align_bytes=64)
         nc.sync.dma_start(out=w2_raw[:], in_=w2.rearrange("(p j) m -> p j m", j=PACK))
 
+        spark = keep.tile([P, 1], F32, name="spark")
+        nc.vector.memset(spark[:], 0.0)
+        spark_out = keep.tile([P, 1], F32, name="spark_out")
+        nc.scalar.activation(spark_out[:], spark[:], RELU)
         ident = keep.tile([P, P], F32, name="ident")
         make_identity(nc, ident[:])
 

@@ -125,5 +125,5 @@ def tile_picked_shuffle_mlp_relu_perm_l_kernel(tc, xT, w1, w2, offs, out):
             done = [keep.tile([P, P], F32, name=f"done{e}{b}") for b in range(2)]
             nc.scalar.copy(done[0][:], res[0][:])
             nc.vector.tensor_copy(done[1][:], res[1][:])
-            nc.scalar.dma_start(out=out_rows[:, 0, block(e)], in_=done[0][:])
+            nc.sync.dma_start(out=out_rows[:, 0, block(e)], in_=done[0][:])
             nc.sync.dma_start(out=out_rows[:, 1, block(e)], in_=done[1][:])

@@ -17,7 +17,7 @@ FP8X4 = mybir.dt.float8_e4m3fn_x4
 RELU = mybir.ActivationFunctionType.Relu
 COPY = mybir.ActivationFunctionType.Copy
 
-LIST_ON_VECTOR = (16, 16)
+LIST_ON_VECTOR = (18, 16)
 
 
 def tile_picked_shuffle_mlp_relu_perm_l_kernel(tc, xT, w1, w2, offs, out):
@@ -32,15 +32,15 @@ def tile_picked_shuffle_mlp_relu_perm_l_kernel(tc, xT, w1, w2, offs, out):
 
         offsets = keep.tile([P, H // 16], U16, name="offsets")
         w1_rows = w1.rearrange("(p j) c -> p j c", j=PACK)
-        w1_upper = keep.tile([P, 2, H], F32, name="w1_upper")
-        nc.sync.dma_start(out=w1_upper[:], in_=w1_rows[:, 0:2, :])
-        w1_lower = [keep.tile([P, 2, H // 2], F32, name=f"w1_lower{a}") for a in range(2)]
-        nc.sync.dma_start(out=w1_lower[0][:], in_=w1_rows[:, 2:4, block(0, H // 2)])
+        w1_left = keep.tile([P, PACK, H // 2], F32, name="w1_left")
+        nc.sync.dma_start(out=w1_left[:], in_=w1_rows[:, :, block(0, H // 2)])
         x_raw = keep.tile([P, PACK, T], F32, name="x_raw")
         nc.sync.dma_start(out=x_raw[:], in_=xT.rearrange("(p j) t -> p j t", j=PACK))
-        nc.sync.dma_start(out=w1_lower[1][:], in_=w1_rows[:, 2:4, block(1, H // 2)])
+        w1_right = [keep.tile([P, 2, H // 2], F32, name="w1_right0"), shared.tile([P, 2, H // 2], F32, name="w1_right1", offset=0, align_bytes=64)]
+        for a in range(2):
+            nc.sync.dma_start(out=w1_right[a][:], in_=w1_rows[:, block(a, 2), block(1, H // 2)])
         nc.sync.dma_start(offsets[:], offs)
-        w2_raw = shared.tile([P, PACK, N], F32, name="w2_raw", offset=0, align_bytes=64)
+        w2_raw = keep.tile([P, PACK, N], F32, name="w2_raw")
         nc.sync.dma_start(out=w2_raw[:], in_=w2.rearrange("(p j) m -> p j m", j=PACK))
 
         spark = keep.tile([P, 1], F32, name="spark")
@@ -68,40 +68,41 @@ def tile_picked_shuffle_mlp_relu_perm_l_kernel(tc, xT, w1, w2, offs, out):
 
         w1_mx = mx_tiles("w1", H)
         x_mx = mx_tiles("x", T)
-        interleave(nc.vector.tensor_copy, w1_mx[0], w1_upper, block(0, 2), 0, 344)
-        interleave(nc.scalar.copy, w1_mx[0], w1_upper, block(0, 2), 344, H)
-        interleave(nc.vector.tensor_copy, w1_mx[0], w1_lower[0], block(1, 2), 0, 176)
-        interleave(nc.scalar.copy, w1_mx[0], w1_lower[0], block(1, 2), 176, 256)
+        interleave(nc.vector.tensor_copy, w1_mx[0], w1_left, block(0, PACK), 0, 176)
+        interleave(nc.scalar.copy, w1_mx[0], w1_left, block(0, PACK), 176, 256)
         quantise(w1_mx, block(0, 256))
         interleave(nc.vector.tensor_copy, x_mx[0], x_raw, block(0, PACK), 0, 96)
         interleave(nc.scalar.copy, x_mx[0], x_raw, block(0, PACK), 96, P)
         interleave(nc.vector.tensor_copy, x_mx[0], x_raw, block(0, PACK), P, 192)
         interleave(nc.scalar.copy, x_mx[0], x_raw, block(0, PACK), 192, T)
         quantise(x_mx, block(0))
-        right = w1_mx[0][:, block(1, H // 2), :]
-        interleave(nc.vector.tensor_copy, right, w1_lower[1], block(1, 2), 0, P)
-        interleave(nc.scalar.copy, right, w1_lower[1], block(1, 2), P, 2 * P)
         quantise(x_mx, block(1))
+        right = w1_mx[0][:, block(1, H // 2), :]
+        interleave(nc.vector.tensor_copy, right, w1_right[0], block(0, 2), 0, P)
+        interleave(nc.scalar.copy, right, w1_right[0], block(0, 2), P, 2 * P)
+        interleave(nc.vector.tensor_copy, right, w1_right[1], block(1, 2), 0, 64)
+        interleave(nc.scalar.copy, right, w1_right[1], block(1, 2), 64, P)
+        interleave(nc.vector.tensor_copy, right, w1_right[1], block(1, 2), P, 224)
+        interleave(nc.scalar.copy, right, w1_right[1], block(1, 2), 224, 2 * P)
         quantise(w1_mx, block(2))
         quantise(w1_mx, block(3))
 
-        h = [keep.tile([P, H], BF16, name=f"h{e}") for e in range(2)]
+        h = [shared.tile([P, H], BF16, name=f"h{e}", offset=2 * H * (1 - e), align_bytes=64) for e in range(2)]
         spans = [slice(0, 256), slice(256, 384), slice(384, 512)]
         prod0 = [psum.tile([P, s.stop - s.start], F32, name=f"prod0{i}", tag=f"bank{i}") for i, s in enumerate(spans)]
         prod1 = [psum.tile([P, H // 2], F32, name=f"prod1{a}", tag=f"bank{3 + a}") for a in range(2)]
-        for i, s in enumerate(spans):
-            product(prod0[i][:], x_mx, block(0), w1_mx, s)
-            product(prod1[0][:] if i == 0 else prod1[1][:, block(i - 1)], x_mx, block(1), w1_mx, s)
+        product(prod0[0][:], x_mx, block(0), w1_mx, spans[0])
+        product(prod1[0][:], x_mx, block(1), w1_mx, spans[0])
+        product(prod0[1][:], x_mx, block(0), w1_mx, spans[1])
+        product(prod0[2][:], x_mx, block(0), w1_mx, spans[2])
+        product(prod1[1][:], x_mx, block(1), w1_mx, block(1, H // 2))
         nc.scalar.activation(h[0][:, spans[0]], prod0[0][:], RELU)
         nc.scalar.activation(h[1][:, block(0, H // 2)], prod1[0][:], RELU)
-        nc.scalar.activation(h[0][:, spans[1]], prod0[1][:], RELU)
+        nc.vector.tensor_relu(h[0][:, spans[1]], prod0[1][:])
         nc.scalar.activation(h[0][:, spans[2]], prod0[2][:], RELU)
         nc.scalar.activation(h[1][:, block(1, H // 2)], prod1[1][:], RELU)
 
-        w2_mx = mx_tiles("w2", N)
-        interleave(nc.vector.tensor_copy, w2_mx[0], w2_raw, block(0, PACK), 0, N)
-
-        picked = [shared.tile([P, H], BF16, name=f"picked{e}", offset=2 * H * e, align_bytes=64) for e in range(2)]
+        picked = [keep.tile([P, H], BF16, name=f"picked{e}", align_bytes=64) for e in range(2)]
         turned = [psum.tile([P, 2, P], F32, name=f"turned{e}", tag=f"bank{6 + e}") for e in range(2)]
         for e in range(2):
             cut = LIST_ON_VECTOR[e]
@@ -109,6 +110,12 @@ def tile_picked_shuffle_mlp_relu_perm_l_kernel(tc, xT, w1, w2, offs, out):
             nc.scalar.activation(picked[e][:, 16 * cut :], h[e][:].indirect(offsets[:, cut:]), COPY)
             for u in range(2):
                 nc.tensor.transpose(turned[e][:, u, :], picked[e][:].bitcast(F32)[:, u : H // 2 : 2], ident[:])
+        w2_grouped = shared.tile([P, N, PACK], BF16, name="w2_grouped", offset=2 * H, align_bytes=64)
+        w2_codes = keep.tile([P, N], U32, name="w2_codes", align_bytes=64)
+        w2_scales = keep.tile([P, N], U8, name="w2_scales", align_bytes=64)
+        w2_mx = (w2_grouped, w2_codes, w2_scales)
+        interleave(nc.vector.tensor_copy, w2_grouped, w2_raw, block(0, PACK), 0, 176)
+        interleave(nc.scalar.copy, w2_grouped, w2_raw, block(0, PACK), 176, N)
         quantise(w2_mx, block(0, N))
 
         h_mx = [mx_tiles(f"h{e}", P) for e in range(2)]

@@ -129,8 +129,7 @@ def tile_picked_shuffle_mlp_relu_perm_l_kernel(tc, xT, w1, w2, offs, out):
             res = [psum.tile([P, P], F32, name=f"res{e}{b}", tag=f"bank{2 * e + b}") for b in range(2)]
             for b in range(2):
                 product(res[b][:], w2_mx, block(b), h_mx[e], block(0))
-            done = [keep.tile([P, P], F32, name=f"done{e}{b}") for b in range(2)]
-            nc.scalar.copy(done[0][:], res[0][:])
-            nc.vector.tensor_copy(done[1][:], res[1][:])
-            nc.sync.dma_start(out=out_rows[:, 0, block(e)], in_=done[0][:])
-            nc.sync.dma_start(out=out_rows[:, 1, block(e)], in_=done[1][:])
+            done = keep.tile([P, 2, P], F32, name=f"done{e}")
+            nc.scalar.copy(done[:, 0, :], res[0][:])
+            nc.vector.tensor_copy(done[:, 1, :], res[1][:])
+            nc.sync.dma_start(out=out_rows[:, :, block(e)], in_=done[:])

@@ -36,9 +36,8 @@ def tile_picked_shuffle_mlp_relu_perm_l_kernel(tc, xT, w1, w2, offs, out):
         nc.sync.dma_start(out=w1_left[:], in_=w1_rows[:, :, block(0, H // 2)])
         x_raw = keep.tile([P, PACK, T], F32, name="x_raw")
         nc.sync.dma_start(out=x_raw[:], in_=xT.rearrange("(p j) t -> p j t", j=PACK))
-        w1_right = [keep.tile([P, 2, H // 2], F32, name="w1_right0"), shared.tile([P, 2, H // 2], F32, name="w1_right1", offset=0, align_bytes=64)]
-        for a in range(2):
-            nc.sync.dma_start(out=w1_right[a][:], in_=w1_rows[:, block(a, 2), block(1, H // 2)])
+        w1_right = shared.tile([P, PACK, H // 2], F32, name="w1_right", offset=0, align_bytes=64)
+        nc.sync.dma_start(out=w1_right[:], in_=w1_rows[:, :, block(1, H // 2)])
         nc.sync.dma_start(offsets[:], offs)
         w2_raw = keep.tile([P, PACK, N], F32, name="w2_raw")
         nc.sync.dma_start(out=w2_raw[:], in_=w2.rearrange("(p j) m -> p j m", j=PACK))
@@ -78,12 +77,10 @@ def tile_picked_shuffle_mlp_relu_perm_l_kernel(tc, xT, w1, w2, offs, out):
         quantise(x_mx, block(0))
         quantise(x_mx, block(1))
         right = w1_mx[0][:, block(1, H // 2), :]
-        interleave(nc.vector.tensor_copy, right, w1_right[0], block(0, 2), 0, P)
-        interleave(nc.scalar.copy, right, w1_right[0], block(0, 2), P, 2 * P)
-        interleave(nc.vector.tensor_copy, right, w1_right[1], block(1, 2), 0, 64)
-        interleave(nc.scalar.copy, right, w1_right[1], block(1, 2), 64, P)
-        interleave(nc.vector.tensor_copy, right, w1_right[1], block(1, 2), P, 224)
-        interleave(nc.scalar.copy, right, w1_right[1], block(1, 2), 224, 2 * P)
+        interleave(nc.vector.tensor_copy, right, w1_right, block(0, PACK), 0, 64)
+        interleave(nc.scalar.copy, right, w1_right, block(0, PACK), 64, P)
+        interleave(nc.vector.tensor_copy, right, w1_right, block(0, PACK), P, 224)
+        interleave(nc.scalar.copy, right, w1_right, block(0, PACK), 224, 2 * P)
         quantise(w1_mx, block(2))
         quantise(w1_mx, block(3))
 
@@ -130,6 +127,7 @@ def tile_picked_shuffle_mlp_relu_perm_l_kernel(tc, xT, w1, w2, offs, out):
             for b in range(2):
                 product(res[b][:], w2_mx, block(b), h_mx[e], block(0))
             done = keep.tile([P, 2, P], F32, name=f"done{e}")
-            nc.scalar.copy(done[:, 0, :], res[0][:])
-            nc.vector.tensor_copy(done[:, 1, :], res[1][:])
-            nc.sync.dma_start(out=out_rows[:, :, block(e)], in_=done[:])
+            for b in range(2):
+                (nc.scalar.copy, nc.vector.tensor_copy)[e](done[:, b, :], res[b][:])
+            for rows in ([slice(0, 2)], [slice(0, 1), slice(1, 2)])[e]:
+                nc.sync.dma_start(out=out_rows[:, rows, block(e)], in_=done[:, rows, :])

@@ -77,10 +77,10 @@ def tile_picked_shuffle_mlp_relu_perm_l_kernel(tc, xT, w1, w2, offs, out):
         quantise(x_mx, block(0))
         quantise(x_mx, block(1))
         right = w1_mx[0][:, block(1, H // 2), :]
-        interleave(nc.vector.tensor_copy, right, w1_right, block(0, PACK), 0, 64)
-        interleave(nc.scalar.copy, right, w1_right, block(0, PACK), 64, P)
-        interleave(nc.vector.tensor_copy, right, w1_right, block(0, PACK), P, 224)
-        interleave(nc.scalar.copy, right, w1_right, block(0, PACK), 224, 2 * P)
+        interleave(nc.vector.tensor_copy, right, w1_right, block(0, PACK), 0, 80)
+        interleave(nc.scalar.copy, right, w1_right, block(0, PACK), 80, P)
+        interleave(nc.vector.tensor_copy, right, w1_right, block(0, PACK), P, 208)
+        interleave(nc.scalar.copy, right, w1_right, block(0, PACK), 208, 2 * P)
         quantise(w1_mx, block(2))
         quantise(w1_mx, block(3))
 
@@ -118,11 +118,13 @@ def tile_picked_shuffle_mlp_relu_perm_l_kernel(tc, xT, w1, w2, offs, out):
         h_mx = [mx_tiles(f"h{e}", P) for e in range(2)]
         for e in range(2):
             words = h_mx[e][0][:].rearrange("p n t -> p (n t)").bitcast(F32).rearrange("p (n u) -> p n u", u=2)
-            nc.scalar.copy(words, turned[e][:].rearrange("p u n -> p n u"))
+            for a in range(2):
+                nc.scalar.copy(words[:, block(a, P // 2), :], turned[e][:, :, block(a, P // 2)].rearrange("p u n -> p n u"))
 
         out_rows = out.rearrange("(b m) t -> m b t", b=2)
         for e in range(2):
-            quantise(h_mx[e], block(0))
+            for a in range(2):
+                quantise(h_mx[e], block(a, P // 2))
             res = [psum.tile([P, P], F32, name=f"res{e}{b}", tag=f"bank{2 * e + b}") for b in range(2)]
             for b in range(2):
                 product(res[b][:], w2_mx, block(b), h_mx[e], block(0))

@@ -50,7 +50,7 @@ def tile_picked_shuffle_mlp_relu_perm_l_kernel(tc, xT, w1, w2, offs, out):
         make_identity(nc, ident[:])
 
         def interleave(copy, grouped, raw, js, c0, c1):
-            copy(grouped[:, c0:c1, js].rearrange("p (c i) j -> p c j i", i=4), raw[:, :, c0:c1].rearrange("p j (c i) -> p c j i", i=4))
+            copy(grouped[:, c0:c1, js].rearrange("p (c i) (u v) -> p c u i v", i=4, v=2), raw[:, :, c0:c1].rearrange("p (u v) (c i) -> p c u i v", i=4, v=2))
 
         def mx_tiles(name, width):
             grouped = keep.tile([P, width, PACK], BF16, name=f"{name}_grouped", align_bytes=64)
@@ -130,6 +130,6 @@ def tile_picked_shuffle_mlp_relu_perm_l_kernel(tc, xT, w1, w2, offs, out):
                 product(res[b][:], w2_mx, block(b), h_mx[e], block(0))
             done = keep.tile([P, 2, P], F32, name=f"done{e}")
             for b in range(2):
-                (nc.scalar.copy, nc.vector.tensor_copy)[e](done[:, b, :], res[b][:])
+                (nc.vector.tensor_copy, nc.scalar.copy)[e](done[:, b, :], res[b][:])
             for rows in ([slice(0, 2)], [slice(0, 1), slice(1, 2)])[e]:
                 nc.sync.dma_start(out=out_rows[:, rows, block(e)], in_=done[:, rows, :])

@@ -34,13 +34,11 @@ def tile_picked_shuffle_mlp_relu_perm_l_kernel(tc, xT, w1, w2, offs, out):
         w1_rows = w1.rearrange("(p j) c -> p j c", j=PACK)
         w1_left = keep.tile([P, PACK, H // 2], F32, name="w1_left")
         nc.sync.dma_start(out=w1_left[:], in_=w1_rows[:, :, block(0, H // 2)])
-        x_raw = keep.tile([P, PACK, T], F32, name="x_raw")
+        x_raw = shared.tile([P, PACK, T], F32, name="x_raw", offset=8 * H, align_bytes=64)
         nc.sync.dma_start(out=x_raw[:], in_=xT.rearrange("(p j) t -> p j t", j=PACK))
         w1_right = shared.tile([P, PACK, H // 2], F32, name="w1_right", offset=0, align_bytes=64)
         nc.sync.dma_start(out=w1_right[:], in_=w1_rows[:, :, block(1, H // 2)])
         nc.sync.dma_start(offsets[:], offs)
-        w2_raw = keep.tile([P, PACK, N], F32, name="w2_raw")
-        nc.sync.dma_start(out=w2_raw[:], in_=w2.rearrange("(p j) m -> p j m", j=PACK))
 
         spark = keep.tile([P, 1], F32, name="spark")
         nc.vector.memset(spark[:], 0.0)
@@ -76,6 +74,8 @@ def tile_picked_shuffle_mlp_relu_perm_l_kernel(tc, xT, w1, w2, offs, out):
         interleave(nc.scalar.copy, x_mx[0], x_raw, block(0, PACK), 192, T)
         quantise(x_mx, block(0))
         quantise(x_mx, block(1))
+        w2_raw = shared.tile([P, PACK, N], F32, name="w2_raw", offset=8 * H, align_bytes=64)
+        nc.sync.dma_start(out=w2_raw[:], in_=w2.rearrange("(p j) m -> p j m", j=PACK))
         right = w1_mx[0][:, block(1, H // 2), :]
         interleave(nc.vector.tensor_copy, right, w1_right, block(0, PACK), 0, 80)
         interleave(nc.scalar.copy, right, w1_right, block(0, PACK), 80, P)

@@ -32,11 +32,11 @@ def tile_picked_shuffle_mlp_relu_perm_l_kernel(tc, xT, w1, w2, offs, out):
 
         offsets = keep.tile([P, H // 16], U16, name="offsets")
         w1_rows = w1.rearrange("(p j) c -> p j c", j=PACK)
-        w1_left = keep.tile([P, PACK, H // 2], F32, name="w1_left")
+        w1_left = keep.tile([P, PACK, H // 2], F32, name="w1_left", align_bytes=256)
         nc.sync.dma_start(out=w1_left[:], in_=w1_rows[:, :, block(0, H // 2)])
-        x_raw = shared.tile([P, PACK, T], F32, name="x_raw", offset=8 * H, align_bytes=64)
+        x_raw = shared.tile([P, PACK, T], F32, name="x_raw", offset=8 * H, align_bytes=256)
         nc.sync.dma_start(out=x_raw[:], in_=xT.rearrange("(p j) t -> p j t", j=PACK))
-        w1_right = shared.tile([P, PACK, H // 2], F32, name="w1_right", offset=0, align_bytes=64)
+        w1_right = shared.tile([P, PACK, H // 2], F32, name="w1_right", offset=0, align_bytes=256)
         nc.sync.dma_start(out=w1_right[:], in_=w1_rows[:, :, block(1, H // 2)])
         nc.sync.dma_start(offsets[:], offs)
 
@@ -74,7 +74,7 @@ def tile_picked_shuffle_mlp_relu_perm_l_kernel(tc, xT, w1, w2, offs, out):
         interleave(nc.scalar.copy, x_mx[0], x_raw, block(0, PACK), 192, T)
         quantise(x_mx, block(0))
         quantise(x_mx, block(1))
-        w2_raw = shared.tile([P, PACK, N], F32, name="w2_raw", offset=8 * H, align_bytes=64)
+        w2_raw = shared.tile([P, PACK, N], F32, name="w2_raw", offset=8 * H, align_bytes=256)
         nc.sync.dma_start(out=w2_raw[:], in_=w2.rearrange("(p j) m -> p j m", j=PACK))
         right = w1_mx[0][:, block(1, H // 2), :]
         interleave(nc.vector.tensor_copy, right, w1_right, block(0, PACK), 0, 80)
@@ -128,7 +128,7 @@ def tile_picked_shuffle_mlp_relu_perm_l_kernel(tc, xT, w1, w2, offs, out):
             res = [psum.tile([P, P], F32, name=f"res{e}{b}", tag=f"bank{2 * e + b}") for b in range(2)]
             for b in range(2):
                 product(res[b][:], w2_mx, block(b), h_mx[e], block(0))
-            done = keep.tile([P, 2, P], F32, name=f"done{e}")
+            done = keep.tile([P, 2, P], F32, name=f"done{e}", align_bytes=256)
             for b in range(2):
                 (nc.vector.tensor_copy, nc.scalar.copy)[e](done[:, b, :], res[b][:])
             for rows in ([slice(0, 2)], [slice(0, 1), slice(1, 2)])[e]:

@@ -130,6 +130,6 @@ def tile_picked_shuffle_mlp_relu_perm_l_kernel(tc, xT, w1, w2, offs, out):
                 product(res[b][:], w2_mx, block(b), h_mx[e], block(0))
             done = keep.tile([P, 2, P], F32, name=f"done{e}", align_bytes=256)
             for b in range(2):
-                (nc.vector.tensor_copy, nc.scalar.copy)[e](done[:, b, :], res[b][:])
+                (nc.vector.tensor_copy if e == 1 and b == 1 else nc.scalar.copy)(done[:, b, :], res[b][:])
             for rows in ([slice(0, 2)], [slice(0, 1), slice(1, 2)])[e]:
                 nc.sync.dma_start(out=out_rows[:, rows, block(e)], in_=done[:, rows, :])

@@ -130,6 +130,6 @@ def tile_picked_shuffle_mlp_relu_perm_l_kernel(tc, xT, w1, w2, offs, out):
                 product(res[b][:], w2_mx, block(b), h_mx[e], block(0))
             done = keep.tile([P, 2, P], F32, name=f"done{e}", align_bytes=256)
             for b in range(2):
-                (nc.vector.tensor_copy if e == 1 and b == 1 else nc.scalar.copy)(done[:, b, :], res[b][:])
+                (nc.scalar.copy, nc.vector.tensor_copy)[e](done[:, b, :], res[b][:])
             for rows in ([slice(0, 2)], [slice(0, 1), slice(1, 2)])[e]:
                 nc.sync.dma_start(out=out_rows[:, rows, block(e)], in_=done[:, rows, :])

@@ -36,8 +36,10 @@ def tile_picked_shuffle_mlp_relu_perm_l_kernel(tc, xT, w1, w2, offs, out):
         nc.sync.dma_start(out=w1_left[:], in_=w1_rows[:, :, block(0, H // 2)])
         x_raw = shared.tile([P, PACK, T], F32, name="x_raw", offset=8 * H, align_bytes=256)
         nc.sync.dma_start(out=x_raw[:], in_=xT.rearrange("(p j) t -> p j t", j=PACK))
-        w1_right = shared.tile([P, PACK, H // 2], F32, name="w1_right", offset=0, align_bytes=256)
-        nc.sync.dma_start(out=w1_right[:], in_=w1_rows[:, :, block(1, H // 2)])
+        w1_third = keep.tile([P, PACK, P], F32, name="w1_third", align_bytes=256)
+        nc.sync.dma_start(out=w1_third[:], in_=w1_rows[:, :, block(2)])
+        w1_last = shared.tile([P, PACK, P], F32, name="w1_last", offset=0, align_bytes=256)
+        nc.sync.dma_start(out=w1_last[:], in_=w1_rows[:, :, block(3)])
         nc.sync.dma_start(offsets[:], offs)
 
         spark = keep.tile([P, 1], F32, name="spark")
@@ -76,11 +78,10 @@ def tile_picked_shuffle_mlp_relu_perm_l_kernel(tc, xT, w1, w2, offs, out):
         quantise(x_mx, block(1))
         w2_raw = shared.tile([P, PACK, N], F32, name="w2_raw", offset=8 * H, align_bytes=256)
         nc.sync.dma_start(out=w2_raw[:], in_=w2.rearrange("(p j) m -> p j m", j=PACK))
-        right = w1_mx[0][:, block(1, H // 2), :]
-        interleave(nc.vector.tensor_copy, right, w1_right, block(0, PACK), 0, 80)
-        interleave(nc.scalar.copy, right, w1_right, block(0, PACK), 80, P)
-        interleave(nc.vector.tensor_copy, right, w1_right, block(0, PACK), P, 208)
-        interleave(nc.scalar.copy, right, w1_right, block(0, PACK), 208, 2 * P)
+        interleave(nc.vector.tensor_copy, w1_mx[0][:, block(2), :], w1_third, block(0, PACK), 0, 32)
+        interleave(nc.scalar.copy, w1_mx[0][:, block(2), :], w1_third, block(0, PACK), 32, P)
+        interleave(nc.vector.tensor_copy, w1_mx[0][:, block(3), :], w1_last, block(0, PACK), 0, 80)
+        interleave(nc.scalar.copy, w1_mx[0][:, block(3), :], w1_last, block(0, PACK), 80, P)
         quantise(w1_mx, block(2))
         quantise(w1_mx, block(3))
 
@@ -131,5 +132,4 @@ def tile_picked_shuffle_mlp_relu_perm_l_kernel(tc, xT, w1, w2, offs, out):
             done = keep.tile([P, 2, P], F32, name=f"done{e}", align_bytes=256)
             for b in range(2):
                 (nc.scalar.copy, nc.vector.tensor_copy)[e](done[:, b, :], res[b][:])
-            for rows in ([slice(0, 2)], [slice(0, 1), slice(1, 2)])[e]:
-                nc.sync.dma_start(out=out_rows[:, rows, block(e)], in_=done[:, rows, :])
+            nc.sync.dma_start(out=out_rows[:, :, block(e)], in_=done[:])

@@ -17,7 +17,7 @@ FP8X4 = mybir.dt.float8_e4m3fn_x4
 RELU = mybir.ActivationFunctionType.Relu
 COPY = mybir.ActivationFunctionType.Copy
 
-LIST_ON_VECTOR = (18, 16)
+LIST_ON_VECTOR = (16, 16)
 
 
 def tile_picked_shuffle_mlp_relu_perm_l_kernel(tc, xT, w1, w2, offs, out):
@@ -86,19 +86,14 @@ def tile_picked_shuffle_mlp_relu_perm_l_kernel(tc, xT, w1, w2, offs, out):
         quantise(w1_mx, block(3))
 
         h = [shared.tile([P, H], BF16, name=f"h{e}", offset=2 * H * (1 - e), align_bytes=64) for e in range(2)]
-        spans = [slice(0, 256), slice(256, 384), slice(384, 512)]
-        prod0 = [psum.tile([P, s.stop - s.start], F32, name=f"prod0{i}", tag=f"bank{i}") for i, s in enumerate(spans)]
-        prod1 = [psum.tile([P, H // 2], F32, name=f"prod1{a}", tag=f"bank{3 + a}") for a in range(2)]
-        product(prod0[0][:], x_mx, block(0), w1_mx, spans[0])
-        product(prod1[0][:], x_mx, block(1), w1_mx, spans[0])
-        product(prod0[1][:], x_mx, block(0), w1_mx, spans[1])
-        product(prod0[2][:], x_mx, block(0), w1_mx, spans[2])
-        product(prod1[1][:], x_mx, block(1), w1_mx, block(1, H // 2))
-        nc.scalar.activation(h[0][:, spans[0]], prod0[0][:], RELU)
-        nc.scalar.activation(h[1][:, block(0, H // 2)], prod1[0][:], RELU)
-        nc.vector.tensor_relu(h[0][:, spans[1]], prod0[1][:])
-        nc.scalar.activation(h[0][:, spans[2]], prod0[2][:], RELU)
-        nc.scalar.activation(h[1][:, block(1, H // 2)], prod1[1][:], RELU)
+        passes = [(e, s) for s in (block(0, H // 2), block(2), block(3)) for e in range(2)]
+        for i, (e, s) in enumerate(passes):
+            prod = psum.tile([P, s.stop - s.start], F32, name=f"prod{i}", tag=f"bank{i}")
+            product(prod[:], x_mx, block(e), w1_mx, s)
+            if s == block(2) or (e == 1 and s == block(3)):
+                nc.vector.tensor_relu(h[e][:, s], prod[:])
+            else:
+                nc.scalar.activation(h[e][:, s], prod[:], RELU)
 
         picked = [keep.tile([P, H], BF16, name=f"picked{e}", align_bytes=64) for e in range(2)]
         turned = [psum.tile([P, 2, P], F32, name=f"turned{e}", tag=f"bank{6 + e}") for e in range(2)]

@@ -80,17 +80,18 @@ def tile_picked_shuffle_mlp_relu_perm_l_kernel(tc, xT, w1, w2, offs, out):
         nc.sync.dma_start(out=w2_raw[:], in_=w2.rearrange("(p j) m -> p j m", j=PACK))
         interleave(nc.vector.tensor_copy, w1_mx[0][:, block(2), :], w1_third, block(0, PACK), 0, 32)
         interleave(nc.scalar.copy, w1_mx[0][:, block(2), :], w1_third, block(0, PACK), 32, P)
-        interleave(nc.vector.tensor_copy, w1_mx[0][:, block(3), :], w1_last, block(0, PACK), 0, 80)
-        interleave(nc.scalar.copy, w1_mx[0][:, block(3), :], w1_last, block(0, PACK), 80, P)
+        interleave(nc.vector.tensor_copy, w1_mx[0][:, block(3), :], w1_last, block(0, PACK), 0, 64)
+        interleave(nc.scalar.copy, w1_mx[0][:, block(3), :], w1_last, block(0, PACK), 64, P)
         quantise(w1_mx, block(2))
-        quantise(w1_mx, block(3))
+        quantise(w1_mx, block(6, 64))
+        quantise(w1_mx, block(7, 64))
 
         h = [shared.tile([P, H], BF16, name=f"h{e}", offset=2 * H * (1 - e), align_bytes=64) for e in range(2)]
         passes = [(e, s) for s in (block(0, H // 2), block(2), block(3)) for e in range(2)]
         for i, (e, s) in enumerate(passes):
             prod = psum.tile([P, s.stop - s.start], F32, name=f"prod{i}", tag=f"bank{i}")
             product(prod[:], x_mx, block(e), w1_mx, s)
-            if s == block(2) or (e == 1 and s == block(3)):
+            if s == block(2):
                 nc.vector.tensor_relu(h[e][:, s], prod[:])
             else:
                 nc.scalar.activation(h[e][:, s], prod[:], RELU)
@@ -118,13 +119,17 @@ def tile_picked_shuffle_mlp_relu_perm_l_kernel(tc, xT, w1, w2, offs, out):
                 nc.scalar.copy(words[:, block(a, P // 2), :], turned[e][:, :, block(a, P // 2)].rearrange("p u n -> p n u"))
 
         out_rows = out.rearrange("(b m) t -> m b t", b=2)
+        whole, halves = block(0), [block(a, P // 2) for a in range(2)]
+        pieces = [
+            [(0, whole, nc.scalar.copy), (1, whole, nc.scalar.copy)],
+            [(0, halves[0], nc.scalar.copy), (1, whole, nc.vector.tensor_copy), (0, halves[1], nc.scalar.copy)],
+        ]
         for e in range(2):
             for a in range(2):
                 quantise(h_mx[e], block(a, P // 2))
-            res = [psum.tile([P, P], F32, name=f"res{e}{b}", tag=f"bank{2 * e + b}") for b in range(2)]
-            for b in range(2):
-                product(res[b][:], w2_mx, block(b), h_mx[e], block(0))
             done = keep.tile([P, 2, P], F32, name=f"done{e}", align_bytes=256)
-            for b in range(2):
-                (nc.scalar.copy, nc.vector.tensor_copy)[e](done[:, b, :], res[b][:])
+            for i, (b, tokens, copy) in enumerate(pieces[e]):
+                res = psum.tile([P, tokens.stop - tokens.start], F32, name=f"res{e}{i}", tag=f"bank{2 * e + i}")
+                product(res[:], w2_mx, block(b), h_mx[e], tokens)
+                copy(done[:, b, tokens], res[:])
             nc.sync.dma_start(out=out_rows[:, :, block(e)], in_=done[:])

@@ -65,7 +65,7 @@ def tile_picked_shuffle_mlp_relu_perm_l_kernel(tc, xT, w1, w2, offs, out):
         def product(res, lhs, lhs_cols, rhs, rhs_cols):
             nc.tensor.matmul_mx(out=res, lhsT=lhs[1][:, lhs_cols].bitcast(FP8X4), lhsT_scale=lhs[2][:, lhs_cols], rhs=rhs[1][:, rhs_cols].bitcast(FP8X4), rhs_scale=rhs[2][:, rhs_cols], start=True, stop=True)
 
-        w1_mx = mx_tiles("w1", H)
+        w1_mx = (shared.tile([P, H, PACK], BF16, name="w1_rounded", offset=16 * H, align_bytes=64),) + mx_tiles("w1", H)[1:]
         x_mx = mx_tiles("x", T)
         interleave(nc.vector.tensor_copy, w1_mx[0], w1_left, block(0, PACK), 0, 176)
         interleave(nc.scalar.copy, w1_mx[0], w1_left, block(0, PACK), 176, 256)
@@ -86,18 +86,18 @@ def tile_picked_shuffle_mlp_relu_perm_l_kernel(tc, xT, w1, w2, offs, out):
         quantise(w1_mx, block(6, 64))
         quantise(w1_mx, block(7, 64))
 
-        h = [shared.tile([P, H], BF16, name=f"h{e}", offset=2 * H * (1 - e), align_bytes=64) for e in range(2)]
-        passes = [(e, s) for s in (block(0, H // 2), block(2), block(3)) for e in range(2)]
+        h = [shared.tile([P, H], BF16, name=f"h{e}", offset=(2 * H, 16 * H)[e], align_bytes=64) for e in range(2)]
+        passes = [(0, block(0, H // 2)), (1, block(0, H // 2)), (0, block(2)), (1, block(2)), (0, block(6, 64)), (0, block(7, 64)), (1, block(3))]
         for i, (e, s) in enumerate(passes):
-            prod = psum.tile([P, s.stop - s.start], F32, name=f"prod{i}", tag=f"bank{i}")
+            prod = psum.tile([P, s.stop - s.start], F32, name=f"prod{i}", tag=f"bank{(0, 1, 2, 3, 4, 5, 6)[i]}")
             product(prod[:], x_mx, block(e), w1_mx, s)
-            if s == block(2):
+            if e == 1:
                 nc.vector.tensor_relu(h[e][:, s], prod[:])
             else:
                 nc.scalar.activation(h[e][:, s], prod[:], RELU)
 
         picked = [keep.tile([P, H], BF16, name=f"picked{e}", align_bytes=64) for e in range(2)]
-        turned = [psum.tile([P, 2, P], F32, name=f"turned{e}", tag=f"bank{6 + e}") for e in range(2)]
+        turned = [psum.tile([P, 2, P], F32, name=f"turned{e}", tag=f"bank{(7, 0)[e]}") for e in range(2)]
         for e in range(2):
             cut = LIST_ON_VECTOR[e]
             nc.vector.tensor_copy(picked[e][:, : 16 * cut], h[e][:].indirect(offsets[:, :cut]))
@@ -129,7 +129,7 @@ def tile_picked_shuffle_mlp_relu_perm_l_kernel(tc, xT, w1, w2, offs, out):
                 quantise(h_mx[e], block(a, P // 2))
             done = keep.tile([P, 2, P], F32, name=f"done{e}", align_bytes=256)
             for i, (b, tokens, copy) in enumerate(pieces[e]):
-                res = psum.tile([P, tokens.stop - tokens.start], F32, name=f"res{e}{i}", tag=f"bank{2 * e + i}")
+                res = psum.tile([P, tokens.stop - tokens.start], F32, name=f"res{e}{i}", tag=f"bank{1 + 2 * e + i}")
                 product(res[:], w2_mx, block(b), h_mx[e], tokens)
                 copy(done[:, b, tokens], res[:])
             nc.sync.dma_start(out=out_rows[:, :, block(e)], in_=done[:])

from contextlib import ExitStack

import concourse.mybir as mybir
from concourse.masks import make_identity

K, T, H, N = 512, 256, 512, 256
P = 128
PACK = 4
FLOPS = 2 * K * H * T + 2 * H * N * T

F32 = mybir.dt.float32
BF16 = mybir.dt.bfloat16
U32 = mybir.dt.uint32
U16 = mybir.dt.uint16
U8 = mybir.dt.uint8
FP8X4 = mybir.dt.float8_e4m3fn_x4
RELU = mybir.ActivationFunctionType.Relu
COPY = mybir.ActivationFunctionType.Copy

LIST_ON_VECTOR = (16, 16)


def tile_picked_shuffle_mlp_relu_perm_l_kernel(tc, xT, w1, w2, offs, out):
    nc = tc.nc
    with ExitStack() as ctx:
        keep = ctx.enter_context(tc.tile_pool(name="keep", bufs=1))
        shared = ctx.enter_context(tc.tile_pool(name="shared", bufs=1))
        psum = ctx.enter_context(tc.psum_pool(name="psum", bufs=1))

        def block(i, width=P):
            return slice(i * width, (i + 1) * width)

        offsets = keep.tile([P, H // 16], U16, name="offsets")
        w1_rows = w1.rearrange("(p j) c -> p j c", j=PACK)
        w1_left = keep.tile([P, PACK, H // 2], F32, name="w1_left", align_bytes=256)
        nc.sync.dma_start(out=w1_left[:], in_=w1_rows[:, :, block(0, H // 2)])
        x_raw = shared.tile([P, PACK, T], F32, name="x_raw", offset=8 * H, align_bytes=256)
        nc.sync.dma_start(out=x_raw[:], in_=xT.rearrange("(p j) t -> p j t", j=PACK))
        w1_third = keep.tile([P, PACK, P], F32, name="w1_third", align_bytes=256)
        nc.sync.dma_start(out=w1_third[:], in_=w1_rows[:, :, block(2)])
        w1_last = shared.tile([P, PACK, P], F32, name="w1_last", offset=0, align_bytes=256)
        nc.sync.dma_start(out=w1_last[:], in_=w1_rows[:, :, block(3)])
        nc.sync.dma_start(offsets[:], offs)

        spark = keep.tile([P, 1], F32, name="spark")
        nc.vector.memset(spark[:], 0.0)
        spark_out = keep.tile([P, 1], F32, name="spark_out")
        nc.scalar.activation(spark_out[:], spark[:], RELU)
        ident = keep.tile([P, P], F32, name="ident")
        make_identity(nc, ident[:])

        def interleave(copy, grouped, raw, js, c0, c1):
            copy(grouped[:, c0:c1, js].rearrange("p (c i) (u v) -> p c u i v", i=4, v=2), raw[:, :, c0:c1].rearrange("p (u v) (c i) -> p c u i v", i=4, v=2))

        def mx_tiles(name, width):
            grouped = keep.tile([P, width, PACK], BF16, name=f"{name}_grouped", align_bytes=64)
            codes = keep.tile([P, width], U32, name=f"{name}_codes", align_bytes=64)
            scales = keep.tile([P, width], U8, name=f"{name}_scales", align_bytes=64)
            return grouped, codes, scales

        def quantise(mx, cols):
            grouped, codes, scales = mx
            nc.vector.quantize_mx(out=codes[:, cols].bitcast(FP8X4), scales=scales[:, cols], in_=grouped[:, cols, :].rearrange("p c j -> p (c j)"))

        def product(res, lhs, lhs_cols, rhs, rhs_cols):
            nc.tensor.matmul_mx(out=res, lhsT=lhs[1][:, lhs_cols].bitcast(FP8X4), lhsT_scale=lhs[2][:, lhs_cols], rhs=rhs[1][:, rhs_cols].bitcast(FP8X4), rhs_scale=rhs[2][:, rhs_cols], start=True, stop=True)

        w1_mx = (shared.tile([P, H, PACK], BF16, name="w1_rounded", offset=16 * H, align_bytes=64),) + mx_tiles("w1", H)[1:]
        x_mx = mx_tiles("x", T)
        interleave(nc.vector.tensor_copy, w1_mx[0], w1_left, block(0, PACK), 0, 176)
        interleave(nc.scalar.copy, w1_mx[0], w1_left, block(0, PACK), 176, 256)
        quantise(w1_mx, block(0, 256))
        interleave(nc.vector.tensor_copy, x_mx[0], x_raw, block(0, PACK), 0, 96)
        interleave(nc.scalar.copy, x_mx[0], x_raw, block(0, PACK), 96, P)
        interleave(nc.vector.tensor_copy, x_mx[0], x_raw, block(0, PACK), P, 192)
        interleave(nc.scalar.copy, x_mx[0], x_raw, block(0, PACK), 192, T)
        quantise(x_mx, block(0))
        quantise(x_mx, block(1))
        w2_raw = shared.tile([P, PACK, N], F32, name="w2_raw", offset=8 * H, align_bytes=256)
        nc.sync.dma_start(out=w2_raw[:], in_=w2.rearrange("(p j) m -> p j m", j=PACK))
        interleave(nc.vector.tensor_copy, w1_mx[0][:, block(2), :], w1_third, block(0, PACK), 0, 32)
        interleave(nc.scalar.copy, w1_mx[0][:, block(2), :], w1_third, block(0, PACK), 32, P)
        interleave(nc.vector.tensor_copy, w1_mx[0][:, block(3), :], w1_last, block(0, PACK), 0, 64)
        interleave(nc.scalar.copy, w1_mx[0][:, block(3), :], w1_last, block(0, PACK), 64, P)
        quantise(w1_mx, block(2))
        quantise(w1_mx, block(6, 64))
        quantise(w1_mx, block(7, 64))

        h = [shared.tile([P, H], BF16, name=f"h{e}", offset=(2 * H, 16 * H)[e], align_bytes=64) for e in range(2)]
        passes = [(0, block(0, H // 2)), (1, block(0, H // 2)), (0, block(2)), (1, block(2)), (0, block(6, 64)), (0, block(7, 64)), (1, block(3))]
        for i, (e, s) in enumerate(passes):
            prod = psum.tile([P, s.stop - s.start], F32, name=f"prod{i}", tag=f"bank{(0, 1, 2, 3, 4, 5, 6)[i]}")
            product(prod[:], x_mx, block(e), w1_mx, s)
            if e == 1:
                nc.vector.tensor_relu(h[e][:, s], prod[:])
            else:
                nc.scalar.activation(h[e][:, s], prod[:], RELU)

        picked = [keep.tile([P, H], BF16, name=f"picked{e}", align_bytes=64) for e in range(2)]
        turned = [psum.tile([P, 2, P], F32, name=f"turned{e}", tag=f"bank{(7, 0)[e]}") for e in range(2)]
        for e in range(2):
            cut = LIST_ON_VECTOR[e]
            nc.vector.tensor_copy(picked[e][:, : 16 * cut], h[e][:].indirect(offsets[:, :cut]))
            nc.scalar.activation(picked[e][:, 16 * cut :], h[e][:].indirect(offsets[:, cut:]), COPY)
            for u in range(2):
                nc.tensor.transpose(turned[e][:, u, :], picked[e][:].bitcast(F32)[:, u : H // 2 : 2], ident[:])
        w2_grouped = shared.tile([P, N, PACK], BF16, name="w2_grouped", offset=2 * H, align_bytes=64)
        w2_codes = keep.tile([P, N], U32, name="w2_codes", align_bytes=64)
        w2_scales = keep.tile([P, N], U8, name="w2_scales", align_bytes=64)
        w2_mx = (w2_grouped, w2_codes, w2_scales)
        interleave(nc.vector.tensor_copy, w2_grouped, w2_raw, block(0, PACK), 0, 176)
        interleave(nc.scalar.copy, w2_grouped, w2_raw, block(0, PACK), 176, N)
        quantise(w2_mx, block(0, N))

        h_mx = [mx_tiles(f"h{e}", P) for e in range(2)]
        for e in range(2):
            words = h_mx[e][0][:].rearrange("p n t -> p (n t)").bitcast(F32).rearrange("p (n u) -> p n u", u=2)
            for a in range(2):
                nc.scalar.copy(words[:, block(a, P // 2), :], turned[e][:, :, block(a, P // 2)].rearrange("p u n -> p n u"))

        out_rows = out.rearrange("(b m) t -> m b t", b=2)
        whole, halves = block(0), [block(a, P // 2) for a in range(2)]
        pieces = [
            [(0, whole, nc.scalar.copy), (1, whole, nc.scalar.copy)],
            [(0, halves[0], nc.scalar.copy), (1, whole, nc.vector.tensor_copy), (0, halves[1], nc.scalar.copy)],
        ]
        for e in range(2):
            for a in range(2):
                quantise(h_mx[e], block(a, P // 2))
            done = keep.tile([P, 2, P], F32, name=f"done{e}", align_bytes=256)
            for i, (b, tokens, copy) in enumerate(pieces[e]):
                res = psum.tile([P, tokens.stop - tokens.start], F32, name=f"res{e}{i}", tag=f"bank{1 + 2 * e + i}")
                product(res[:], w2_mx, block(b), h_mx[e], tokens)
                copy(done[:, b, tokens], res[:])
            nc.sync.dma_start(out=out_rows[:, :, block(e)], in_=done[:])
